import numpy as np, ml_dtypes
CORES = [33,38,57,62,81,86,161,166,185,190,209,214]
N = 12
QP = 64
def setup_inputs(rng):
    m = 150 * rng.standard_normal((1, QP, 1), dtype=np.float32) + 3 * rng.standard_normal((N, QP, 1), dtype=np.float32)
    m = (m + rng.uniform(100, 300, (1, QP, 1)) * (rng.random((1, QP, 1)) < 0.7) * (rng.random((N, QP, 1)) < 0.5)).astype(np.float32)
    l = 20 * (1 + np.abs(rng.standard_normal((N, QP, 1), dtype=np.float32)))
    return {"o": (l * rng.standard_normal((N, QP, 128), dtype=np.float32) / 4).astype(ml_dtypes.bfloat16), "ml": np.concatenate([m, l], axis=2)}
def setup_inputs_big(rng):
    d = setup_inputs(rng)
    for k in ("o",): d[k] = (d[k].astype(np.float32) * 1048576.0).astype(d[k].dtype)
    return d
def setup_inputs_small(rng):
    d = setup_inputs(rng)
    for k in ("o",): d[k] = (d[k].astype(np.float32) * (1 / 1048576.0)).astype(d[k].dtype)
    return d
def reference(o, ml):
    O, ML = o.astype(np.float64), ml.astype(np.float64)
    m, l = ML[:, :, 0:1], ML[:, :, 1:2]
    f = np.exp(m - m.max(axis=0))
    y = ((f * O).sum(axis=0) / (f * l).sum(axis=0)).astype(ml_dtypes.bfloat16)
    return {"y": np.broadcast_to(y, (N,) + y.shape)}

@@ -1,0 +1,209 @@
+from concourse.bass import DstId, RemoteDMATransfer
+from concourse.mybir import AluOpType, AxisListType, ActivationFunctionType
+
+N, Q, DV, NP = 12, 64, 128, 6
+SIM_CORES = 256
+ORDER = ["C", "1", "6", "D"]
+
+SCRATCH = {
+    "oland": ("dram", [N, 128, 64], "bfloat16"),
+    "mlland": ("dram", [N, 128, 2], "float32"),
+    "S": ("sbuf", [128, NP * DV], "bfloat16"),
+    "Y": ("sbuf", [128, 256], "float32"),
+    "Z": ("sbuf", [128, Q], "float32"),
+    "Ist": ("sbuf", [128, Q], "bfloat16"),
+    "I12": ("sbuf", [128, N], "float32"),
+    "negM": ("sbuf", [128, 4], "float32"),
+    "Fsel": ("sbuf", [128, 8], "float32"),
+    "F12": ("sbuf", [128, N], "float32"),
+    "FL": ("sbuf", [128, N], "float32"),
+    "den": ("sbuf", [128, 4], "float32"),
+    "rden": ("sbuf", [128, 4], "float32"),
+    "W": ("sbuf", [128, NP * Q], "bfloat16"),
+    "ysb": ("sbuf", [128, DV], "bfloat16"),
+    "PSm": ("psum", [128, 512], "float32"),
+    "PSl": ("psum", [128, 512], "float32"),
+    "PSo": ("psum", [128, 512], "float32"),
+}
+SEMAPHORES = (["cz", "cs", "ci", "ce", "mlld", "mlarr", "yld", "pm", "pl", "nm", "fs", "f12", "s1", "s2", "s3", "mm", "yd",
+               "st", "sent", "old", "oH", "oC", "o1", "o6", "oD"]
+              + ["w%d" % k for k in range(NP)] + ["sld%d" % k for k in range(NP)])
+
+
+def _same_chip(topo, a, b):
+    return topo.host(a) == topo.host(b) and topo.chip(a) == topo.chip(b)
+
+
+def _bits(m):
+    return bin(m).count("1")
+
+
+def _plan(cores, topo):
+    n = len(cores)
+    far = {s: [d for d in range(n) if d != s and not topo.may_write(cores[s], cores[d])] for s in range(n)}
+    near = {s: [d for d in range(n) if d != s and topo.may_write(cores[s], cores[d])] for s in range(n)}
+
+    def rot(s, ds):
+        return sorted(ds, key=lambda d: (d - s) % n)
+
+    helpers, job = {}, {}
+    for s in range(n):
+        helpers[s] = []
+        if far[s]:
+            hs = [h for h in range(SIM_CORES)
+                  if h not in cores and _same_chip(topo, h, cores[s]) and topo.die(h) == topo.die(cores[s])
+                  and all(topo.may_write(h, cores[d]) for d in far[s])]
+            helpers[s] = hs
+            ds = rot(s, far[s])
+            for i, h in enumerate(hs):
+                job[h] = (s, ds[i::len(hs)])
+
+    def cls(d, s):
+        if s != d and s in far and d in far[s]:
+            return "D"
+        if s == d or _same_chip(topo, cores[s], cores[d]) or topo.same_plane(cores[s], cores[d]):
+            return "1" if far[s] else "6"
+        return "C"
+
+    slots = {d: sorted(range(n), key=lambda s: (ORDER.index(cls(d, s)), s)) for d in range(n)}
+    mask = {}
+    for s in range(n):
+        m = -1
+        for t in [cores[d] for d in near[s]] + helpers[s]:
+            m &= topo.mask(cores[s], t)
+        mask[cores[s]] = m
+    for h in job:
+        m = -1
+        for d in job[h][1]:
+            m &= topo.mask(h, cores[d])
+        mask[h] = m
+    writer = {}
+    for s in range(n):
+        for d in near[s]:
+            writer[(s, d)] = cores[s]
+    for h in job:
+        for d in job[h][1]:
+            writer[(job[h][0], d)] = h
+    return dict(far=far, near=near, rot=rot, helpers=helpers, job=job, cls=cls, slots=slots, mask=mask, writer=writer)
+
+
+def _send(g, topo, core, src, targets, sem, mask, local):
+    ids = []
+    for t, _ in targets:
+        rid, pid = topo.addr(t, core)
+        ids.append(DstId(rid=rid, pnc=pid))
+    g.remote_dma_fused([RemoteDMATransfer(dst_ids=ids, dma_engine_mask=mask, remote_sem=sem, srcs=[src],
+                                          dsts=[ap for _, ap in targets], alu_op=0)], local_sem=local)
+    return _bits(mask)
+
+
+def rank_program(g, core, T, topo):
+    cores = [int(c) for c in T.cores]
+    P = _plan(cores, topo)
+    sem = T.sem
+    slot = lambda d, s: P["slots"][d].index(s)
+
+    if core in P["job"]:
+        s, ds = P["job"][core]
+        got = _bits(P["mask"][cores[s]])
+        m = P["mask"][core]
+        g.wait_ge(sem.mlarr, got)
+        out = _send(g, topo, core, T.mlland[0], [(cores[d], T.mlland[slot(d, s)]) for d in ds], sem.mlarr, m, sem.sent)
+        g.wait_ge(sem.oH, got)
+        out += _send(g, topo, core, T.oland[0], [(cores[d], T.oland[slot(d, s)]) for d in ds], sem.oD, m, sem.sent)
+        g.wait_ge(sem.sent, out)
+        return
+    r = T.rank_of(core)
+    if r is None:
+        return
+
+    V, A, PE, SY = g.vector, g.scalar, g.tensor, g.sync
+    Exp = ActivationFunctionType.Exp
+    me = slot(r, r)
+    m = P["mask"][core]
+
+    A.dma_start(T.mlland[me, 0:Q, :], T.ml[:]).then_inc(sem.mlld, 16)
+    A.dma_start(T.mlland[me, Q:2 * Q, :], T.ml[:]).then_inc(sem.mlld, 16)
+    SY.dma_start(T.oland[me], T.o[:]).then_inc(sem.old, 16)
+    V.memset(T.Z[:], 0.0).then_inc(sem.cz, 1)
+
+    hs = P["helpers"][r]
+    cross = [d for d in P["rot"](r, P["near"][r]) if P["cls"](d, r) == "C"]
+    same = [d for d in P["rot"](r, P["near"][r]) if P["cls"](d, r) != "C"]
+    g.wait_ge(sem.mlld, 32)
+    out = _send(g, topo, core, T.mlland[me],
+                [(h, T.mlland[0]) for h in hs] + [(cores[d], T.mlland[slot(d, r)]) for d in cross + same],
+                sem.mlarr, m, sem.sent)
+    g.wait_ge(sem.old, 16)
+    if hs:
+        out += _send(g, topo, core, T.oland[me], [(h, T.oland[0]) for h in hs], sem.oH, m, sem.sent)
+    if cross:
+        out += _send(g, topo, core, T.oland[me], [(cores[d], T.oland[slot(d, r)]) for d in cross], sem.oC, m, sem.sent)
+    out += _send(g, topo, core, T.oland[me], [(cores[d], T.oland[slot(d, r)]) for d in same],
+                 sem["o" + P["cls"](r, r)], m, sem.sent)
+
+    g.wait_ge(sem.cz, 1)
+    for h in range(2):
+        g.affine_select(T.Z[h * Q:(h + 1) * Q, :], T.Z[h * Q:(h + 1) * Q, :], [[-1, Q]], AluOpType.is_equal, -30000.0, 0, 1
+                        ).then_inc(sem.cs, 1)
+    V.wait_ge(sem.cs, 2)
+    V.tensor_scalar(T.I12[0:N, :], T.Z[0:N, 0:N], 0.0, None, AluOpType.is_equal).then_inc(sem.ci, 1)
+    A.wait_ge(sem.cs, 2)
+    A.activation(T.Ist[:], T.Z[:], Exp).then_inc(sem.ce, 1)
+
+    others = [s for s in range(N) if s != r]
+    ml_total = sum(_bits(P["mask"][P["writer"][(s, r)]]) for s in others)
+    need = {c: sum(_bits(P["mask"][P["writer"][(s, r)]]) for s in others if P["cls"](r, s) == c) for c in ORDER}
+
+    A.wait_ge(sem.mlld, 32)
+    A.wait_ge(sem.mlarr, ml_total)
+    A.dma_start(T.Y[0:N, :], T.mlland[:]).then_inc(sem.yld, 16)
+
+    for k in range(NP):
+        pair = P["slots"][r][2 * k:2 * k + 2]
+        cl = [P["cls"](r, s) for s in pair]
+        q = A if "D" in cl else SY
+        if r in pair:
+            q.wait_ge(sem.old, 16)
+        for c in sorted(set(cl)):
+            if need[c]:
+                q.wait_ge(sem["o" + c], need[c])
+        q.dma_start(T.S[:, k * DV:(k + 1) * DV], T.oland[2 * k:2 * k + 2]).then_inc(sem["sld%d" % k], 16)
+
+    PE.wait_ge(sem.yld, 16)
+    PE.wait_ge(sem.ci, 1)
+    PE.transpose(T.PSm[:, 0:N], T.Y[0:N, 0:256:2], T.I12[0:N, :]).then_inc(sem.pm, 1)
+    PE.transpose(T.PSl[:, 0:N], T.Y[0:N, 1:256:2], T.I12[0:N, :]).then_inc(sem.pl, 1)
+    V.wait_ge(sem.pm, 1)
+    V.tensor_reduce(T.negM[:, 0:1], T.PSm[:, 0:N], AxisListType.X, AluOpType.max, negate=True).then_inc(sem.nm, 1)
+    A.wait_ge(sem.nm, 1)
+    for h in range(2):
+        A.activation(T.Fsel[h * Q:(h + 1) * Q, 0:NP], T.PSm[h * Q:(h + 1) * Q, h:N:2], Exp,
+                     bias=T.negM[h * Q:(h + 1) * Q, 0:1]).then_inc(sem.fs, 1)
+    A.activation(T.F12[0:Q, :], T.PSm[0:Q, 0:N], Exp, bias=T.negM[0:Q, 0:1]).then_inc(sem.f12, 1)
+    V.wait_ge(sem.fs, 2)
+    V.wait_ge(sem.ce, 1)
+    for k in range(NP):
+        V.tensor_scalar(T.W[:, k * Q:(k + 1) * Q], T.Ist[:], T.Fsel[:, k:k + 1], None, AluOpType.mult
+                        ).then_inc(sem["w%d" % k], 1)
+    V.wait_ge(sem.f12, 1)
+    V.wait_ge(sem.pl, 1)
+    V.tensor_tensor(T.FL[0:Q, :], T.F12[0:Q, :], T.PSl[0:Q, 0:N], AluOpType.mult).then_inc(sem.s1, 1)
+    V.wait_ge(sem.s1, 1)
+    V.tensor_reduce(T.den[0:Q, 0:1], T.FL[0:Q, :], AxisListType.X, AluOpType.add).then_inc(sem.s2, 1)
+    V.wait_ge(sem.s2, 1)
+    V.reciprocal(T.rden[0:Q, 0:1], T.den[0:Q, 0:1]).then_inc(sem.s3, 1)
+
+    for k in range(NP):
+        PE.wait_ge(sem["w%d" % k], 1)
+        PE.wait_ge(sem["sld%d" % k], 16)
+        mm = PE.matmul(T.PSo[0:Q, 0:DV], T.W[:, k * Q:(k + 1) * Q], T.S[:, k * DV:(k + 1) * DV],
+                       start=(k == 0), stop=(k == NP - 1))
+    mm.then_inc(sem.mm, 1)
+    V.wait_ge(sem.s3, 1)
+    V.wait_ge(sem.mm, 1)
+    V.tensor_scalar(T.ysb[0:Q, :], T.PSo[0:Q, 0:DV], T.rden[0:Q, 0:1], None, AluOpType.mult).then_inc(sem.yd, 1)
+    SY.wait_ge(sem.yd, 1)
+    SY.dma_start(T.y[:], T.ysb[0:Q, :]).then_inc(sem.st, 16)
+    SY.wait_ge(sem.st, 16)
+    g.wait_ge(sem.sent, out)

@@ -1,33 +1,40 @@
 from concourse.bass import DstId, RemoteDMATransfer
 from concourse.mybir import AluOpType, AxisListType, ActivationFunctionType
 
-N, Q, DV, NP = 12, 64, 128, 6
+N, Q, DV = 12, 64, 128
+H = DV // 2
+NW = 8
+NRMAX = 4
 SIM_CORES = 256
 ORDER = ["C", "1", "6", "D"]
 
 SCRATCH = {
     "oland": ("dram", [N, 128, 64], "bfloat16"),
     "mlland": ("dram", [N, 128, 2], "float32"),
-    "S": ("sbuf", [128, NP * DV], "bfloat16"),
+    "ohq": ("dram", [128, H], "bfloat16"),
+    "S": ("sbuf", [128, (N // 2) * DV], "bfloat16"),
+    "Sr": ("sbuf", [128, NRMAX * H], "bfloat16"),
+    "MLa": ("sbuf", [128, 2 * N], "float32"),
     "Y": ("sbuf", [128, 256], "float32"),
     "Z": ("sbuf", [128, Q], "float32"),
     "Ist": ("sbuf", [128, Q], "bfloat16"),
     "I12": ("sbuf", [128, N], "float32"),
     "negM": ("sbuf", [128, 4], "float32"),
-    "Fsel": ("sbuf", [128, 8], "float32"),
     "F12": ("sbuf", [128, N], "float32"),
     "FL": ("sbuf", [128, N], "float32"),
     "den": ("sbuf", [128, 4], "float32"),
     "rden": ("sbuf", [128, 4], "float32"),
-    "W": ("sbuf", [128, NP * Q], "bfloat16"),
+    "W": ("sbuf", [128, NW * Q], "bfloat16"),
     "ysb": ("sbuf", [128, DV], "bfloat16"),
     "PSm": ("psum", [128, 512], "float32"),
     "PSl": ("psum", [128, 512], "float32"),
-    "PSo": ("psum", [128, 512], "float32"),
+    "PSa": ("psum", [128, 512], "float32"),
+    "PSb": ("psum", [128, 512], "float32"),
 }
-SEMAPHORES = (["cz", "cs", "ci", "ce", "mlld", "mlarr", "yld", "pm", "pl", "nm", "fs", "f12", "s1", "s2", "s3", "mm", "yd",
-               "st", "sent", "old", "oH", "oC", "o1", "o6", "oD"]
-              + ["w%d" % k for k in range(NP)] + ["sld%d" % k for k in range(NP)])
+SEMAPHORES = (["cz", "cs", "ci", "ce", "mlld", "mlarr", "mlR", "yld", "pm", "pl", "cp", "nm", "f12", "s1", "s2", "s3", "mm",
+               "yd", "st", "sent", "old", "ohl", "oH", "oC", "o1", "o6"]
+              + ["oR%d" % i for i in range(NRMAX)] + ["w%d" % k for k in range(NW)]
+              + ["sld%d" % k for k in range(N // 2)])
 
 
 def _same_chip(topo, a, b):
@@ -46,26 +53,52 @@ def _plan(cores, topo):
     def rot(s, ds):
         return sorted(ds, key=lambda d: (d - s) % n)
 
-    helpers, job = {}, {}
+    idle = [h for h in range(SIM_CORES) if h not in cores]
+    used = set()
+    relay = {}
+
+    def take(s, d, cands, like):
+        free = [h for h in cands if h not in used and topo.may_write(cores[s], h) and topo.may_write(h, cores[d])]
+        free.sort(key=lambda h: (topo.die(h) != topo.die(like), h))
+        if not free:
+            return False
+        used.add(free[0])
+        relay[(s, d)] = free[0]
+        return True
+
+    groups = {}
     for s in range(n):
-        helpers[s] = []
-        if far[s]:
-            hs = [h for h in range(SIM_CORES)
-                  if h not in cores and _same_chip(topo, h, cores[s]) and topo.die(h) == topo.die(cores[s])
-                  and all(topo.may_write(h, cores[d]) for d in far[s])]
-            helpers[s] = hs
-            ds = rot(s, far[s])
-            for i, h in enumerate(hs):
-                job[h] = (s, ds[i::len(hs)])
+        for d in far[s]:
+            groups.setdefault((topo.host(cores[d]), topo.chip(cores[d])), {}).setdefault(s, []).append(d)
+    for key in sorted(groups):
+        by_s = groups[key]
+        alld = [d for s in by_s for d in by_s[s]]
+        cands = [h for h in idle if topo.mates(h, cores[alld[0]]) and all(topo.may_write(h, cores[d]) for d in alld)
+                 and all(topo.may_write(cores[s], h) for s in by_s)]
+        share = len(cands) // len(by_s)
+        for i, s in enumerate(sorted(by_s)):
+            ds = by_s[s]
+            ds = ds[i % len(ds):] + ds[:i % len(ds)]
+            for d in ds[:share]:
+                take(s, d, cands, cores[d])
+    for s in range(n):
+        for d in far[s]:
+            if (s, d) not in relay:
+                ok = take(s, d, [h for h in idle if _same_chip(topo, h, cores[s])], cores[s])
+                assert ok
+
+    helpers = {s: [relay[(s, d)] for d in rot(s, far[s])] for s in range(n)}
+    job = {relay[k]: k for k in relay}
 
     def cls(d, s):
-        if s != d and s in far and d in far[s]:
+        if s != d and d in far[s]:
             return "D"
         if s == d or _same_chip(topo, cores[s], cores[d]) or topo.same_plane(cores[s], cores[d]):
             return "1" if far[s] else "6"
         return "C"
 
     slots = {d: sorted(range(n), key=lambda s: (ORDER.index(cls(d, s)), s)) for d in range(n)}
+    nd = {d: sum(1 for s in range(n) if cls(d, s) != "D") for d in range(n)}
     mask = {}
     for s in range(n):
         m = -1
@@ -73,18 +106,8 @@ def _plan(cores, topo):
             m &= topo.mask(cores[s], t)
         mask[cores[s]] = m
     for h in job:
-        m = -1
-        for d in job[h][1]:
-            m &= topo.mask(h, cores[d])
-        mask[h] = m
-    writer = {}
-    for s in range(n):
-        for d in near[s]:
-            writer[(s, d)] = cores[s]
-    for h in job:
-        for d in job[h][1]:
-            writer[(job[h][0], d)] = h
-    return dict(far=far, near=near, rot=rot, helpers=helpers, job=job, cls=cls, slots=slots, mask=mask, writer=writer)
+        mask[h] = topo.mask(h, cores[job[h][1]])
+    return dict(far=far, near=near, rot=rot, helpers=helpers, job=job, cls=cls, slots=slots, nd=nd, mask=mask)
 
 
 def _send(g, topo, core, src, targets, sem, mask, local):
@@ -104,13 +127,15 @@ def rank_program(g, core, T, topo):
     slot = lambda d, s: P["slots"][d].index(s)
 
     if core in P["job"]:
-        s, ds = P["job"][core]
+        s, d = P["job"][core]
         got = _bits(P["mask"][cores[s]])
         m = P["mask"][core]
+        c = slot(d, s)
+        i = c - P["nd"][d]
         g.wait_ge(sem.mlarr, got)
-        out = _send(g, topo, core, T.mlland[0], [(cores[d], T.mlland[slot(d, s)]) for d in ds], sem.mlarr, m, sem.sent)
+        out = _send(g, topo, core, T.mlland[0], [(cores[d], T.MLa[:, 2 * c:2 * c + 2])], sem.mlR, m, sem.sent)
         g.wait_ge(sem.oH, got)
-        out += _send(g, topo, core, T.oland[0], [(cores[d], T.oland[slot(d, s)]) for d in ds], sem.oD, m, sem.sent)
+        out += _send(g, topo, core, T.ohq[:], [(cores[d], T.Sr[:, i * H:(i + 1) * H])], sem["oR%d" % i], m, sem.sent)
         g.wait_ge(sem.sent, out)
         return
     r = T.rank_of(core)
@@ -118,25 +143,34 @@ def rank_program(g, core, T, topo):
         return
 
     V, A, PE, SY = g.vector, g.scalar, g.tensor, g.sync
-    Exp = ActivationFunctionType.Exp
+    Exp, Copy = ActivationFunctionType.Exp, ActivationFunctionType.Copy
     me = slot(r, r)
     m = P["mask"][core]
+    hs = P["helpers"][r]
+    nd = P["nd"][r]
+    npair, nr = nd // 2, N - nd
+    assert nd % 2 == 0 and nr <= NRMAX and npair + nr <= NW and (2 * nd) % 4 == 0
 
     A.dma_start(T.mlland[me, 0:Q, :], T.ml[:]).then_inc(sem.mlld, 16)
     A.dma_start(T.mlland[me, Q:2 * Q, :], T.ml[:]).then_inc(sem.mlld, 16)
-    SY.dma_start(T.oland[me], T.o[:]).then_inc(sem.old, 16)
+    if hs:
+        SY.dma_start(T.ohq[0:Q, :], T.o[:, 0:H]).then_inc(sem.ohl, 16)
+        SY.dma_start(T.ohq[Q:2 * Q, :], T.o[:, H:DV]).then_inc(sem.ohl, 16)
+        A.dma_start(T.oland[me], T.o[:]).then_inc(sem.old, 16)
+    else:
+        SY.dma_start(T.oland[me], T.o[:]).then_inc(sem.old, 16)
     V.memset(T.Z[:], 0.0).then_inc(sem.cz, 1)
 
-    hs = P["helpers"][r]
     cross = [d for d in P["rot"](r, P["near"][r]) if P["cls"](d, r) == "C"]
     same = [d for d in P["rot"](r, P["near"][r]) if P["cls"](d, r) != "C"]
     g.wait_ge(sem.mlld, 32)
     out = _send(g, topo, core, T.mlland[me],
                 [(h, T.mlland[0]) for h in hs] + [(cores[d], T.mlland[slot(d, r)]) for d in cross + same],
                 sem.mlarr, m, sem.sent)
-    g.wait_ge(sem.old, 16)
     if hs:
-        out += _send(g, topo, core, T.oland[me], [(h, T.oland[0]) for h in hs], sem.oH, m, sem.sent)
+        g.wait_ge(sem.ohl, 32)
+        out += _send(g, topo, core, T.ohq[:], [(h, T.ohq[:]) for h in hs], sem.oH, m, sem.sent)
+    g.wait_ge(sem.old, 16)
     if cross:
         out += _send(g, topo, core, T.oland[me], [(cores[d], T.oland[slot(d, r)]) for d in cross], sem.oC, m, sem.sent)
     out += _send(g, topo, core, T.oland[me], [(cores[d], T.oland[slot(d, r)]) for d in same],
@@ -151,59 +185,90 @@ def rank_program(g, core, T, topo):
     A.wait_ge(sem.cs, 2)
     A.activation(T.Ist[:], T.Z[:], Exp).then_inc(sem.ce, 1)
 
-    others = [s for s in range(N) if s != r]
-    ml_total = sum(_bits(P["mask"][P["writer"][(s, r)]]) for s in others)
-    need = {c: sum(_bits(P["mask"][P["writer"][(s, r)]]) for s in others if P["cls"](r, s) == c) for c in ORDER}
+    direct = [s for s in range(N) if s != r and P["cls"](r, s) != "D"]
+    ml_total = sum(_bits(P["mask"][cores[s]]) for s in direct)
+    need = {c: sum(_bits(P["mask"][cores[s]]) for s in direct if P["cls"](r, s) == c) for c in ORDER}
+    rel = {}
+    for h in P["job"]:
+        s, d = P["job"][h]
+        if d == r:
+            rel[slot(r, s) - nd] = _bits(P["mask"][h])
+    assert sorted(rel) == list(range(nr))
 
-    A.wait_ge(sem.mlld, 32)
-    A.wait_ge(sem.mlarr, ml_total)
-    A.dma_start(T.Y[0:N, :], T.mlland[:]).then_inc(sem.yld, 16)
+    SY.wait_ge(sem.mlld, 32)
+    SY.wait_ge(sem.mlarr, ml_total)
+    SY.dma_start(T.Y[0:nd, 0:128], T.mlland[0:nd, 0:Q, :]).then_inc(sem.yld, 16)
+    SY.dma_start(T.Y[0:nd:2, 128:256], T.mlland[1:nd:2, Q:2 * Q, :]).then_inc(sem.yld, 16)
+    SY.dma_start(T.Y[1:nd:2, 128:256], T.mlland[0:nd:2, Q:2 * Q, :]).then_inc(sem.yld, 16)
 
-    for k in range(NP):
+    for k in range(npair):
         pair = P["slots"][r][2 * k:2 * k + 2]
-        cl = [P["cls"](r, s) for s in pair]
-        q = A if "D" in cl else SY
         if r in pair:
-            q.wait_ge(sem.old, 16)
-        for c in sorted(set(cl)):
+            SY.wait_ge(sem.old, 16)
+        for c in sorted(set(P["cls"](r, s) for s in pair)):
             if need[c]:
-                q.wait_ge(sem["o" + c], need[c])
-        q.dma_start(T.S[:, k * DV:(k + 1) * DV], T.oland[2 * k:2 * k + 2]).then_inc(sem["sld%d" % k], 16)
+                SY.wait_ge(sem["o" + c], need[c])
+        SY.dma_start(T.S[:, k * DV:(k + 1) * DV], T.oland[2 * k:2 * k + 2]).then_inc(sem["sld%d" % k], 16)
 
-    PE.wait_ge(sem.yld, 16)
+    PE.wait_ge(sem.yld, 48)
     PE.wait_ge(sem.ci, 1)
-    PE.transpose(T.PSm[:, 0:N], T.Y[0:N, 0:256:2], T.I12[0:N, :]).then_inc(sem.pm, 1)
-    PE.transpose(T.PSl[:, 0:N], T.Y[0:N, 1:256:2], T.I12[0:N, :]).then_inc(sem.pl, 1)
+    PE.transpose(T.PSm[:, 0:nd], T.Y[0:nd, 0:256:2], T.I12[0:nd, 0:nd]).then_inc(sem.pm, 1)
+    PE.transpose(T.PSl[:, 0:nd], T.Y[0:nd, 1:256:2], T.I12[0:nd, 0:nd]).then_inc(sem.pl, 1)
     V.wait_ge(sem.pm, 1)
-    V.tensor_reduce(T.negM[:, 0:1], T.PSm[:, 0:N], AxisListType.X, AluOpType.max, negate=True).then_inc(sem.nm, 1)
-    A.wait_ge(sem.nm, 1)
-    for h in range(2):
-        A.activation(T.Fsel[h * Q:(h + 1) * Q, 0:NP], T.PSm[h * Q:(h + 1) * Q, h:N:2], Exp,
-                     bias=T.negM[h * Q:(h + 1) * Q, 0:1]).then_inc(sem.fs, 1)
-    A.activation(T.F12[0:Q, :], T.PSm[0:Q, 0:N], Exp, bias=T.negM[0:Q, 0:1]).then_inc(sem.f12, 1)
-    V.wait_ge(sem.fs, 2)
-    V.wait_ge(sem.ce, 1)
-    for k in range(NP):
-        V.tensor_scalar(T.W[:, k * Q:(k + 1) * Q], T.Ist[:], T.Fsel[:, k:k + 1], None, AluOpType.mult
-                        ).then_inc(sem["w%d" % k], 1)
-    V.wait_ge(sem.f12, 1)
+    V.tensor_copy(T.MLa[:, 0:2 * nd:2], T.PSm[:, 0:nd]).then_inc(sem.cp, 1)
     V.wait_ge(sem.pl, 1)
-    V.tensor_tensor(T.FL[0:Q, :], T.F12[0:Q, :], T.PSl[0:Q, 0:N], AluOpType.mult).then_inc(sem.s1, 1)
+    V.tensor_copy(T.MLa[:, 1:2 * nd:2], T.PSl[:, 0:nd]).then_inc(sem.cp, 1)
+
+    mlr = sum(rel.values())
+    V.wait_ge(sem.cp, 2)
+    V.wait_ge(sem.mlR, mlr)
+    V.tensor_reduce(T.negM[:, 0:1], T.MLa[:, 0:2 * N:2], AxisListType.X, AluOpType.max, negate=True).then_inc(sem.nm, 1)
+    A.wait_ge(sem.cp, 2)
+    A.wait_ge(sem.mlR, mlr)
+    A.wait_ge(sem.nm, 1)
+    A.activation(T.F12[:, 0:N], T.MLa[:, 0:2 * N:2], Exp, bias=T.negM[:, 0:1]).then_inc(sem.f12, 1)
+    col = [2 * k for k in range(npair)] + [nd + i for i in range(nr)]
+    nv = 3
+    V.wait_ge(sem.f12, 1)
+    V.wait_ge(sem.ce, 1)
+    A.wait_ge(sem.f12, 1)
+    A.wait_ge(sem.ce, 1)
+    for j in range(npair + nr):
+        if j < nv:
+            V.tensor_scalar(T.W[:, j * Q:(j + 1) * Q], T.Ist[:], T.F12[:, col[j]:col[j] + 1], None, AluOpType.mult
+                            ).then_inc(sem["w%d" % j], 1)
+        else:
+            A.activation(T.W[:, j * Q:(j + 1) * Q], T.Ist[:], Copy, scale=T.F12[:, col[j]:col[j] + 1]
+                         ).then_inc(sem["w%d" % j], 1)
+    V.tensor_tensor(T.FL[0:Q, :], T.F12[0:Q, :], T.MLa[0:Q, 1:2 * N:2], AluOpType.mult).then_inc(sem.s1, 1)
     V.wait_ge(sem.s1, 1)
     V.tensor_reduce(T.den[0:Q, 0:1], T.FL[0:Q, :], AxisListType.X, AluOpType.add).then_inc(sem.s2, 1)
     V.wait_ge(sem.s2, 1)
     V.reciprocal(T.rden[0:Q, 0:1], T.den[0:Q, 0:1]).then_inc(sem.s3, 1)
 
-    for k in range(NP):
+    for k in range(npair):
         PE.wait_ge(sem["w%d" % k], 1)
         PE.wait_ge(sem["sld%d" % k], 16)
-        mm = PE.matmul(T.PSo[0:Q, 0:DV], T.W[:, k * Q:(k + 1) * Q], T.S[:, k * DV:(k + 1) * DV],
-                       start=(k == 0), stop=(k == NP - 1))
-    mm.then_inc(sem.mm, 1)
+        PE.matmul(T.PSa[0:Q, 0:H], T.W[:, k * Q:(k + 1) * Q], T.S[:, k * DV:k * DV + H], start=(k == 0), stop=False)
+        PE.matmul(T.PSb[0:Q, 0:H], T.W[:, k * Q:(k + 1) * Q], T.S[:, k * DV + H:(k + 1) * DV], start=(k == 0), stop=False)
+    for i in range(nr):
+        j = npair + i
+        PE.wait_ge(sem["w%d" % j], 1)
+        PE.wait_ge(sem["oR%d" % i], rel[i])
+        ma = PE.matmul(T.PSa[0:Q, 0:H], T.W[0:Q, j * Q:(j + 1) * Q], T.Sr[0:Q, i * H:(i + 1) * H],
+                       start=False, stop=(i == nr - 1))
+        mb = PE.matmul(T.PSb[0:Q, 0:H], T.W[Q:2 * Q, j * Q:(j + 1) * Q], T.Sr[Q:2 * Q, i * H:(i + 1) * H],
+                       start=False, stop=(i == nr - 1))
+    ma.then_inc(sem.mm, 1)
+    mb.then_inc(sem.mm, 1)
+
     V.wait_ge(sem.s3, 1)
-    V.wait_ge(sem.mm, 1)
-    V.tensor_scalar(T.ysb[0:Q, :], T.PSo[0:Q, 0:DV], T.rden[0:Q, 0:1], None, AluOpType.mult).then_inc(sem.yd, 1)
-    SY.wait_ge(sem.yd, 1)
+    V.wait_ge(sem.mm, 2)
+    V.tensor_scalar(T.ysb[0:Q, 0:H], T.PSa[0:Q, 0:H], T.rden[0:Q, 0:1], None, AluOpType.mult).then_inc(sem.yd, 1)
+    A.wait_ge(sem.s3, 1)
+    A.wait_ge(sem.mm, 2)
+    A.activation(T.ysb[0:Q, H:DV], T.PSb[0:Q, 0:H], Copy, scale=T.rden[0:Q, 0:1]).then_inc(sem.yd, 1)
+    SY.wait_ge(sem.yd, 2)
     SY.dma_start(T.y[:], T.ysb[0:Q, :]).then_inc(sem.st, 16)
     SY.wait_ge(sem.st, 16)
     g.wait_ge(sem.sent, out)

@@ -5,6 +5,7 @@ N, Q, DV = 12, 64, 128
 H = DV // 2
 NW = 8
 NRMAX = 4
+EW = 16
 SIM_CORES = 256
 ORDER = ["C", "1", "6", "D"]
 
@@ -17,6 +18,7 @@ SCRATCH = {
     "MLa": ("sbuf", [128, 2 * N], "float32"),
     "Y": ("sbuf", [128, 256], "float32"),
     "Z": ("sbuf", [128, Q], "float32"),
+    "Za": ("sbuf", [128, Q], "float32"),
     "Ist": ("sbuf", [128, Q], "bfloat16"),
     "I12": ("sbuf", [128, N], "float32"),
     "negM": ("sbuf", [128, 4], "float32"),
@@ -31,8 +33,8 @@ SCRATCH = {
     "PSa": ("psum", [128, 512], "float32"),
     "PSb": ("psum", [128, 512], "float32"),
 }
-SEMAPHORES = (["cz", "cs", "ci", "ce", "mlld", "mlarr", "mlR", "yld", "pm", "pl", "cp", "nm", "f12", "s1", "s2", "s3", "mm",
-               "yd", "st", "sent", "old", "ohl", "oH", "oC", "o1", "o6"]
+SEMAPHORES = (["ci0", "cz", "cv0", "cv1", "ci", "ce", "mlld", "mlarr", "mlR", "yld", "pm", "pl", "cp", "nm", "f12", "s1", "s2",
+               "s3", "mm", "yd", "st", "sent", "old", "ohl", "oH", "oC", "o1", "o6"]
               + ["oR%d" % i for i in range(NRMAX)] + ["w%d" % k for k in range(NW)]
               + ["sld%d" % k for k in range(N // 2)])
 
@@ -43,6 +45,17 @@ def _same_chip(topo, a, b):
 
 def _bits(m):
     return bin(m).count("1")
+
+
+def _part(m, upper):
+    bits = [b for b in range(m.bit_length()) if (m >> b) & 1]
+    sel = bits[len(bits) // 2:] if upper else bits[:len(bits) // 2]
+    return sum(1 << b for b in sel)
+
+
+def _ramp(g, T, a, b):
+    g.iota(T.Z[:, a:b], [[-1, b - a]], -a - Q // 2, 1, allow_small_or_imprecise_dtypes=True).then_inc(T.sem.ci0, 1)
+    g.wait_ge(T.sem.ci0, 1)
 
 
 def _plan(cores, topo):
@@ -107,7 +120,10 @@ def _plan(cores, topo):
         mask[cores[s]] = m
     for h in job:
         mask[h] = topo.mask(h, cores[job[h][1]])
-    return dict(far=far, near=near, rot=rot, helpers=helpers, job=job, cls=cls, slots=slots, nd=nd, mask=mask)
+    mlmask = {cores[s]: _part(mask[cores[s]], False) for s in range(n)}
+    emask = {cores[s]: _part(mask[cores[s]], True) for s in range(n)}
+    return dict(far=far, near=near, rot=rot, helpers=helpers, job=job, cls=cls, slots=slots, nd=nd, mask=mask,
+                mlmask=mlmask, emask=emask)
 
 
 def _send(g, topo, core, src, targets, sem, mask, local):
@@ -128,13 +144,16 @@ def rank_program(g, core, T, topo):
 
     if core in P["job"]:
         s, d = P["job"][core]
-        got = _bits(P["mask"][cores[s]])
         m = P["mask"][core]
         c = slot(d, s)
         i = c - P["nd"][d]
-        g.wait_ge(sem.mlarr, got)
-        out = _send(g, topo, core, T.mlland[0], [(cores[d], T.MLa[:, 2 * c:2 * c + 2])], sem.mlR, m, sem.sent)
-        g.wait_ge(sem.oH, got)
+        k = N - P["nd"][d]
+        a, b = EW + (Q - 2 * EW) * i // k, EW + (Q - 2 * EW) * (i + 1) // k
+        _ramp(g, T, a, b)
+        out = _send(g, topo, core, T.Z[:, a:b], [(cores[d], T.Z[:, a:b])], sem.cz, m, sem.sent)
+        g.wait_ge(sem.mlarr, _bits(P["mlmask"][cores[s]]))
+        out += _send(g, topo, core, T.mlland[0], [(cores[d], T.MLa[:, 2 * c:2 * c + 2])], sem.mlR, m, sem.sent)
+        g.wait_ge(sem.oH, _bits(P["mask"][cores[s]]))
         out += _send(g, topo, core, T.ohq[:], [(cores[d], T.Sr[:, i * H:(i + 1) * H])], sem["oR%d" % i], m, sem.sent)
         g.wait_ge(sem.sent, out)
         return
@@ -159,14 +178,19 @@ def rank_program(g, core, T, topo):
         A.dma_start(T.oland[me], T.o[:]).then_inc(sem.old, 16)
     else:
         SY.dma_start(T.oland[me], T.o[:]).then_inc(sem.old, 16)
-    V.memset(T.Z[:], 0.0).then_inc(sem.cz, 1)
+
+    (pr,) = [x for x in range(N) if x != r and _same_chip(topo, cores[x], core)]
+    a, b = (0, EW) if r < pr else (Q - EW, Q)
+    ra, rb = (EW, Q) if r < pr else (0, Q - EW)
+    _ramp(g, T, a, b)
+    out = _send(g, topo, core, T.Z[:, a:b], [(cores[pr], T.Z[:, a:b])], sem.cz, P["emask"][core], sem.sent)
 
     cross = [d for d in P["rot"](r, P["near"][r]) if P["cls"](d, r) == "C"]
     same = [d for d in P["rot"](r, P["near"][r]) if P["cls"](d, r) != "C"]
     g.wait_ge(sem.mlld, 32)
-    out = _send(g, topo, core, T.mlland[me],
-                [(h, T.mlland[0]) for h in hs] + [(cores[d], T.mlland[slot(d, r)]) for d in cross + same],
-                sem.mlarr, m, sem.sent)
+    out += _send(g, topo, core, T.mlland[me],
+                 [(h, T.mlland[0]) for h in hs] + [(cores[d], T.mlland[slot(d, r)]) for d in cross + same],
+                 sem.mlarr, P["mlmask"][core], sem.sent)
     if hs:
         g.wait_ge(sem.ohl, 32)
         out += _send(g, topo, core, T.ohq[:], [(h, T.ohq[:]) for h in hs], sem.oH, m, sem.sent)
@@ -176,17 +200,8 @@ def rank_program(g, core, T, topo):
     out += _send(g, topo, core, T.oland[me], [(cores[d], T.oland[slot(d, r)]) for d in same],
                  sem["o" + P["cls"](r, r)], m, sem.sent)
 
-    g.wait_ge(sem.cz, 1)
-    for h in range(2):
-        g.affine_select(T.Z[h * Q:(h + 1) * Q, :], T.Z[h * Q:(h + 1) * Q, :], [[-1, Q]], AluOpType.is_equal, -30000.0, 0, 1
-                        ).then_inc(sem.cs, 1)
-    V.wait_ge(sem.cs, 2)
-    V.tensor_scalar(T.I12[0:N, :], T.Z[0:N, 0:N], 0.0, None, AluOpType.is_equal).then_inc(sem.ci, 1)
-    A.wait_ge(sem.cs, 2)
-    A.activation(T.Ist[:], T.Z[:], Exp).then_inc(sem.ce, 1)
-
     direct = [s for s in range(N) if s != r and P["cls"](r, s) != "D"]
-    ml_total = sum(_bits(P["mask"][cores[s]]) for s in direct)
+    ml_total = sum(_bits(P["mlmask"][cores[s]]) for s in direct)
     need = {c: sum(_bits(P["mask"][cores[s]]) for s in direct if P["cls"](r, s) == c) for c in ORDER}
     rel = {}
     for h in P["job"]:
@@ -194,6 +209,20 @@ def rank_program(g, core, T, topo):
         if d == r:
             rel[slot(r, s) - nd] = _bits(P["mask"][h])
     assert sorted(rel) == list(range(nr))
+
+    hq2 = float((Q // 2) ** 2)
+    for n_, (x, y_) in enumerate([(a, b), (ra, rb)]):
+        cv = sem["cv%d" % n_]
+        if n_ == 0:
+            V.wait_ge(sem.ci0, 1)
+        else:
+            V.wait_ge(sem.cz, _bits(P["emask"][cores[pr]]) + sum(rel.values()))
+        V.tensor_tensor(T.Za[:, x:y_], T.Z[:, x:y_], T.Z[:, x:y_], AluOpType.mult).then_inc(cv, 1)
+        V.wait_ge(cv, 1)
+        V.tensor_scalar(T.Za[:, x:y_], T.Za[:, x:y_], hq2, -30000.0, AluOpType.not_equal, AluOpType.mult).then_inc(cv, 1)
+        A.wait_ge(cv, 2)
+        A.activation(T.Ist[:, x:y_], T.Za[:, x:y_], Exp).then_inc(sem.ce, 1)
+    V.tensor_scalar(T.I12[0:N, :], T.Z[0:N, 0:N], float(-(Q // 2)), None, AluOpType.is_equal).then_inc(sem.ci, 1)
 
     SY.wait_ge(sem.mlld, 32)
     SY.wait_ge(sem.mlarr, ml_total)
@@ -230,9 +259,9 @@ def rank_program(g, core, T, topo):
     col = [2 * k for k in range(npair)] + [nd + i for i in range(nr)]
     nv = 3
     V.wait_ge(sem.f12, 1)
-    V.wait_ge(sem.ce, 1)
+    V.wait_ge(sem.ce, 2)
     A.wait_ge(sem.f12, 1)
-    A.wait_ge(sem.ce, 1)
+    A.wait_ge(sem.ce, 2)
     for j in range(npair + nr):
         if j < nv:
             V.tensor_scalar(T.W[:, j * Q:(j + 1) * Q], T.Ist[:], T.F12[:, col[j]:col[j] + 1], None, AluOpType.mult

from concourse.bass import DstId, RemoteDMATransfer
from concourse.mybir import AluOpType, AxisListType, ActivationFunctionType

N, Q, DV = 12, 64, 128
H = DV // 2
NW = 8
NRMAX = 4
EW = 16
SIM_CORES = 256
ORDER = ["C", "1", "6", "D"]

SCRATCH = {
    "oland": ("dram", [N, 128, 64], "bfloat16"),
    "mlland": ("dram", [N, 128, 2], "float32"),
    "ohq": ("dram", [128, H], "bfloat16"),
    "S": ("sbuf", [128, (N // 2) * DV], "bfloat16"),
    "Sr": ("sbuf", [128, NRMAX * H], "bfloat16"),
    "MLa": ("sbuf", [128, 2 * N], "float32"),
    "Y": ("sbuf", [128, 256], "float32"),
    "Z": ("sbuf", [128, Q], "float32"),
    "Za": ("sbuf", [128, Q], "float32"),
    "Ist": ("sbuf", [128, Q], "bfloat16"),
    "I12": ("sbuf", [128, N], "float32"),
    "negM": ("sbuf", [128, 4], "float32"),
    "F12": ("sbuf", [128, N], "float32"),
    "FL": ("sbuf", [128, N], "float32"),
    "den": ("sbuf", [128, 4], "float32"),
    "rden": ("sbuf", [128, 4], "float32"),
    "W": ("sbuf", [128, NW * Q], "bfloat16"),
    "ysb": ("sbuf", [128, DV], "bfloat16"),
    "PSm": ("psum", [128, 512], "float32"),
    "PSl": ("psum", [128, 512], "float32"),
    "PSa": ("psum", [128, 512], "float32"),
    "PSb": ("psum", [128, 512], "float32"),
}
SEMAPHORES = (["ci0", "cz", "cv0", "cv1", "ci", "ce", "mlld", "mlarr", "mlR", "yld", "pm", "pl", "cp", "nm", "f12", "s1", "s2",
               "s3", "mm", "yd", "st", "sent", "old", "ohl", "oH", "oC", "o1", "o6"]
              + ["oR%d" % i for i in range(NRMAX)] + ["w%d" % k for k in range(NW)]
              + ["sld%d" % k for k in range(N // 2)])


def _same_chip(topo, a, b):
    return topo.host(a) == topo.host(b) and topo.chip(a) == topo.chip(b)


def _bits(m):
    return bin(m).count("1")


def _part(m, upper):
    bits = [b for b in range(m.bit_length()) if (m >> b) & 1]
    sel = bits[len(bits) // 2:] if upper else bits[:len(bits) // 2]
    return sum(1 << b for b in sel)


def _ramp(g, T, a, b):
    g.iota(T.Z[:, a:b], [[-1, b - a]], -a - Q // 2, 1, allow_small_or_imprecise_dtypes=True).then_inc(T.sem.ci0, 1)
    g.wait_ge(T.sem.ci0, 1)


def _plan(cores, topo):
    n = len(cores)
    far = {s: [d for d in range(n) if d != s and not topo.may_write(cores[s], cores[d])] for s in range(n)}
    near = {s: [d for d in range(n) if d != s and topo.may_write(cores[s], cores[d])] for s in range(n)}

    def rot(s, ds):
        return sorted(ds, key=lambda d: (d - s) % n)

    idle = [h for h in range(SIM_CORES) if h not in cores]
    used = set()
    relay = {}

    def take(s, d, cands, like):
        free = [h for h in cands if h not in used and topo.may_write(cores[s], h) and topo.may_write(h, cores[d])]
        free.sort(key=lambda h: (topo.die(h) != topo.die(like), h))
        if not free:
            return False
        used.add(free[0])
        relay[(s, d)] = free[0]
        return True

    groups = {}
    for s in range(n):
        for d in far[s]:
            groups.setdefault((topo.host(cores[d]), topo.chip(cores[d])), {}).setdefault(s, []).append(d)
    for key in sorted(groups):
        by_s = groups[key]
        alld = [d for s in by_s for d in by_s[s]]
        cands = [h for h in idle if topo.mates(h, cores[alld[0]]) and all(topo.may_write(h, cores[d]) for d in alld)
                 and all(topo.may_write(cores[s], h) for s in by_s)]
        share = len(cands) // len(by_s)
        for i, s in enumerate(sorted(by_s)):
            ds = by_s[s]
            ds = ds[i % len(ds):] + ds[:i % len(ds)]
            for d in ds[:share]:
                take(s, d, cands, cores[d])
    for s in range(n):
        for d in far[s]:
            if (s, d) not in relay:
                ok = take(s, d, [h for h in idle if _same_chip(topo, h, cores[s])], cores[s])
                assert ok

    helpers = {s: [relay[(s, d)] for d in rot(s, far[s])] for s in range(n)}
    job = {relay[k]: k for k in relay}

    def cls(d, s):
        if s != d and d in far[s]:
            return "D"
        if s == d or _same_chip(topo, cores[s], cores[d]) or topo.same_plane(cores[s], cores[d]):
            return "1" if far[s] else "6"
        return "C"

    slots = {d: sorted(range(n), key=lambda s: (ORDER.index(cls(d, s)), s)) for d in range(n)}
    nd = {d: sum(1 for s in range(n) if cls(d, s) != "D") for d in range(n)}
    mask = {}
    for s in range(n):
        m = -1
        for t in [cores[d] for d in near[s]] + helpers[s]:
            m &= topo.mask(cores[s], t)
        mask[cores[s]] = m
    for h in job:
        mask[h] = topo.mask(h, cores[job[h][1]])
    mlmask = {cores[s]: _part(mask[cores[s]], False) for s in range(n)}
    emask = {cores[s]: _part(mask[cores[s]], True) for s in range(n)}
    return dict(far=far, near=near, rot=rot, helpers=helpers, job=job, cls=cls, slots=slots, nd=nd, mask=mask,
                mlmask=mlmask, emask=emask)


def _send(g, topo, core, src, targets, sem, mask, local):
    ids = []
    for t, _ in targets:
        rid, pid = topo.addr(t, core)
        ids.append(DstId(rid=rid, pnc=pid))
    g.remote_dma_fused([RemoteDMATransfer(dst_ids=ids, dma_engine_mask=mask, remote_sem=sem, srcs=[src],
                                          dsts=[ap for _, ap in targets], alu_op=0)], local_sem=local)
    return _bits(mask)


def rank_program(g, core, T, topo):
    cores = [int(c) for c in T.cores]
    P = _plan(cores, topo)
    sem = T.sem
    slot = lambda d, s: P["slots"][d].index(s)

    if core in P["job"]:
        s, d = P["job"][core]
        m = P["mask"][core]
        c = slot(d, s)
        i = c - P["nd"][d]
        k = N - P["nd"][d]
        a, b = EW + (Q - 2 * EW) * i // k, EW + (Q - 2 * EW) * (i + 1) // k
        _ramp(g, T, a, b)
        out = _send(g, topo, core, T.Z[:, a:b], [(cores[d], T.Z[:, a:b])], sem.cz, m, sem.sent)
        g.wait_ge(sem.mlarr, _bits(P["mlmask"][cores[s]]))
        out += _send(g, topo, core, T.mlland[0], [(cores[d], T.MLa[:, 2 * c:2 * c + 2])], sem.mlR, m, sem.sent)
        g.wait_ge(sem.oH, _bits(P["mask"][cores[s]]))
        out += _send(g, topo, core, T.ohq[:], [(cores[d], T.Sr[:, i * H:(i + 1) * H])], sem["oR%d" % i], m, sem.sent)
        g.wait_ge(sem.sent, out)
        return
    r = T.rank_of(core)
    if r is None:
        return

    V, A, PE, SY = g.vector, g.scalar, g.tensor, g.sync
    Exp, Copy = ActivationFunctionType.Exp, ActivationFunctionType.Copy
    me = slot(r, r)
    m = P["mask"][core]
    hs = P["helpers"][r]
    nd = P["nd"][r]
    npair, nr = nd // 2, N - nd
    assert nd % 2 == 0 and nr <= NRMAX and npair + nr <= NW and (2 * nd) % 4 == 0

    A.dma_start(T.mlland[me, 0:Q, :], T.ml[:]).then_inc(sem.mlld, 16)
    A.dma_start(T.mlland[me, Q:2 * Q, :], T.ml[:]).then_inc(sem.mlld, 16)
    if hs:
        SY.dma_start(T.ohq[0:Q, :], T.o[:, 0:H]).then_inc(sem.ohl, 16)
        SY.dma_start(T.ohq[Q:2 * Q, :], T.o[:, H:DV]).then_inc(sem.ohl, 16)
        A.dma_start(T.oland[me], T.o[:]).then_inc(sem.old, 16)
    else:
        SY.dma_start(T.oland[me], T.o[:]).then_inc(sem.old, 16)

    (pr,) = [x for x in range(N) if x != r and _same_chip(topo, cores[x], core)]
    a, b = (0, EW) if r < pr else (Q - EW, Q)
    ra, rb = (EW, Q) if r < pr else (0, Q - EW)
    _ramp(g, T, a, b)
    out = _send(g, topo, core, T.Z[:, a:b], [(cores[pr], T.Z[:, a:b])], sem.cz, P["emask"][core], sem.sent)

    cross = [d for d in P["rot"](r, P["near"][r]) if P["cls"](d, r) == "C"]
    same = [d for d in P["rot"](r, P["near"][r]) if P["cls"](d, r) != "C"]
    g.wait_ge(sem.mlld, 32)
    out += _send(g, topo, core, T.mlland[me],
                 [(h, T.mlland[0]) for h in hs] + [(cores[d], T.mlland[slot(d, r)]) for d in cross + same],
                 sem.mlarr, P["mlmask"][core], sem.sent)
    if hs:
        g.wait_ge(sem.ohl, 32)
        out += _send(g, topo, core, T.ohq[:], [(h, T.ohq[:]) for h in hs], sem.oH, m, sem.sent)
    g.wait_ge(sem.old, 16)
    if cross:
        out += _send(g, topo, core, T.oland[me], [(cores[d], T.oland[slot(d, r)]) for d in cross], sem.oC, m, sem.sent)
    out += _send(g, topo, core, T.oland[me], [(cores[d], T.oland[slot(d, r)]) for d in same],
                 sem["o" + P["cls"](r, r)], m, sem.sent)

    direct = [s for s in range(N) if s != r and P["cls"](r, s) != "D"]
    ml_total = sum(_bits(P["mlmask"][cores[s]]) for s in direct)
    need = {c: sum(_bits(P["mask"][cores[s]]) for s in direct if P["cls"](r, s) == c) for c in ORDER}
    rel = {}
    for h in P["job"]:
        s, d = P["job"][h]
        if d == r:
            rel[slot(r, s) - nd] = _bits(P["mask"][h])
    assert sorted(rel) == list(range(nr))

    hq2 = float((Q // 2) ** 2)
    for n_, (x, y_) in enumerate([(a, b), (ra, rb)]):
        cv = sem["cv%d" % n_]
        if n_ == 0:
            V.wait_ge(sem.ci0, 1)
        else:
            V.wait_ge(sem.cz, _bits(P["emask"][cores[pr]]) + sum(rel.values()))
        V.tensor_tensor(T.Za[:, x:y_], T.Z[:, x:y_], T.Z[:, x:y_], AluOpType.mult).then_inc(cv, 1)
        V.wait_ge(cv, 1)
        V.tensor_scalar(T.Za[:, x:y_], T.Za[:, x:y_], hq2, -30000.0, AluOpType.not_equal, AluOpType.mult).then_inc(cv, 1)
        A.wait_ge(cv, 2)
        A.activation(T.Ist[:, x:y_], T.Za[:, x:y_], Exp).then_inc(sem.ce, 1)
    V.tensor_scalar(T.I12[0:N, :], T.Z[0:N, 0:N], float(-(Q // 2)), None, AluOpType.is_equal).then_inc(sem.ci, 1)

    SY.wait_ge(sem.mlld, 32)
    SY.wait_ge(sem.mlarr, ml_total)
    SY.dma_start(T.Y[0:nd, 0:128], T.mlland[0:nd, 0:Q, :]).then_inc(sem.yld, 16)
    SY.dma_start(T.Y[0:nd:2, 128:256], T.mlland[1:nd:2, Q:2 * Q, :]).then_inc(sem.yld, 16)
    SY.dma_start(T.Y[1:nd:2, 128:256], T.mlland[0:nd:2, Q:2 * Q, :]).then_inc(sem.yld, 16)

    for k in range(npair):
        pair = P["slots"][r][2 * k:2 * k + 2]
        if r in pair:
            SY.wait_ge(sem.old, 16)
        for c in sorted(set(P["cls"](r, s) for s in pair)):
            if need[c]:
                SY.wait_ge(sem["o" + c], need[c])
        SY.dma_start(T.S[:, k * DV:(k + 1) * DV], T.oland[2 * k:2 * k + 2]).then_inc(sem["sld%d" % k], 16)

    PE.wait_ge(sem.yld, 48)
    PE.wait_ge(sem.ci, 1)
    PE.transpose(T.PSm[:, 0:nd], T.Y[0:nd, 0:256:2], T.I12[0:nd, 0:nd]).then_inc(sem.pm, 1)
    PE.transpose(T.PSl[:, 0:nd], T.Y[0:nd, 1:256:2], T.I12[0:nd, 0:nd]).then_inc(sem.pl, 1)
    V.wait_ge(sem.pm, 1)
    V.tensor_copy(T.MLa[:, 0:2 * nd:2], T.PSm[:, 0:nd]).then_inc(sem.cp, 1)
    V.wait_ge(sem.pl, 1)
    V.tensor_copy(T.MLa[:, 1:2 * nd:2], T.PSl[:, 0:nd]).then_inc(sem.cp, 1)

    mlr = sum(rel.values())
    V.wait_ge(sem.cp, 2)
    V.wait_ge(sem.mlR, mlr)
    V.tensor_reduce(T.negM[:, 0:1], T.MLa[:, 0:2 * N:2], AxisListType.X, AluOpType.max, negate=True).then_inc(sem.nm, 1)
    A.wait_ge(sem.cp, 2)
    A.wait_ge(sem.mlR, mlr)
    A.wait_ge(sem.nm, 1)
    A.activation(T.F12[:, 0:N], T.MLa[:, 0:2 * N:2], Exp, bias=T.negM[:, 0:1]).then_inc(sem.f12, 1)
    col = [2 * k for k in range(npair)] + [nd + i for i in range(nr)]
    nv = 3
    V.wait_ge(sem.f12, 1)
    V.wait_ge(sem.ce, 2)
    A.wait_ge(sem.f12, 1)
    A.wait_ge(sem.ce, 2)
    for j in range(npair + nr):
        if j < nv:
            V.tensor_scalar(T.W[:, j * Q:(j + 1) * Q], T.Ist[:], T.F12[:, col[j]:col[j] + 1], None, AluOpType.mult
                            ).then_inc(sem["w%d" % j], 1)
        else:
            A.activation(T.W[:, j * Q:(j + 1) * Q], T.Ist[:], Copy, scale=T.F12[:, col[j]:col[j] + 1]
                         ).then_inc(sem["w%d" % j], 1)
    V.tensor_tensor(T.FL[0:Q, :], T.F12[0:Q, :], T.MLa[0:Q, 1:2 * N:2], AluOpType.mult).then_inc(sem.s1, 1)
    V.wait_ge(sem.s1, 1)
    V.tensor_reduce(T.den[0:Q, 0:1], T.FL[0:Q, :], AxisListType.X, AluOpType.add).then_inc(sem.s2, 1)
    V.wait_ge(sem.s2, 1)
    V.reciprocal(T.rden[0:Q, 0:1], T.den[0:Q, 0:1]).then_inc(sem.s3, 1)

    for k in range(npair):
        PE.wait_ge(sem["w%d" % k], 1)
        PE.wait_ge(sem["sld%d" % k], 16)
        PE.matmul(T.PSa[0:Q, 0:H], T.W[:, k * Q:(k + 1) * Q], T.S[:, k * DV:k * DV + H], start=(k == 0), stop=False)
        PE.matmul(T.PSb[0:Q, 0:H], T.W[:, k * Q:(k + 1) * Q], T.S[:, k * DV + H:(k + 1) * DV], start=(k == 0), stop=False)
    for i in range(nr):
        j = npair + i
        PE.wait_ge(sem["w%d" % j], 1)
        PE.wait_ge(sem["oR%d" % i], rel[i])
        ma = PE.matmul(T.PSa[0:Q, 0:H], T.W[0:Q, j * Q:(j + 1) * Q], T.Sr[0:Q, i * H:(i + 1) * H],
                       start=False, stop=(i == nr - 1))
        mb = PE.matmul(T.PSb[0:Q, 0:H], T.W[Q:2 * Q, j * Q:(j + 1) * Q], T.Sr[Q:2 * Q, i * H:(i + 1) * H],
                       start=False, stop=(i == nr - 1))
    ma.then_inc(sem.mm, 1)
    mb.then_inc(sem.mm, 1)

    V.wait_ge(sem.s3, 1)
    V.wait_ge(sem.mm, 2)
    V.tensor_scalar(T.ysb[0:Q, 0:H], T.PSa[0:Q, 0:H], T.rden[0:Q, 0:1], None, AluOpType.mult).then_inc(sem.yd, 1)
    A.wait_ge(sem.s3, 1)
    A.wait_ge(sem.mm, 2)
    A.activation(T.ysb[0:Q, H:DV], T.PSb[0:Q, 0:H], Copy, scale=T.rden[0:Q, 0:1]).then_inc(sem.yd, 1)
    SY.wait_ge(sem.yd, 2)
    SY.dma_start(T.y[:], T.ysb[0:Q, :]).then_inc(sem.st, 16)
    SY.wait_ge(sem.st, 16)
    g.wait_ge(sem.sent, out)
